import numpy as np
import ml_dtypes


def mxq(x, axis, fmt="e4m3"):
    dtype, down = {"e4m3": (ml_dtypes.float8_e4m3fn, 7), "e5m2": (ml_dtypes.float8_e5m2, 14)}[fmt]
    v = np.moveaxis(np.asarray(x, np.float32).astype(ml_dtypes.bfloat16).astype(np.float64), axis, -1)
    blocks = v.reshape(v.shape[:-1] + (-1, 32))
    amax = np.abs(blocks).max(-1, keepdims=True)
    byte = np.maximum(np.where(amax > 0, np.frexp(amax)[1] - 1 + 127, 0) - down, 1)
    scale = np.exp2(byte - 127.0)
    codes = (blocks / scale).astype(np.float32).astype(dtype).astype(np.float64)
    return np.moveaxis((codes * scale).reshape(v.shape), -1, axis)


WIDE = False


def mx_kscale(k):
    if not WIDE:
        return np.ones(k)
    levels = np.array([10, -10, 5, -5, 0])
    if k % 512:
        return np.exp2(np.random.permutation(np.resize(levels, k // 32))).repeat(32)
    a = np.empty((k // 512, 16))
    for p in range(k // 512):
        a[p, :8] = np.random.permutation(np.resize(levels, 8))
        for g in range(8):
            far = levels[np.abs(levels - a[p, g]) >= 10]
            a[p, g + 8] = far[np.random.randint(len(far))]
    return np.exp2(a.ravel()).repeat(32)


def f64(x):
    return np.asarray(x).astype(np.float64)


def striped8(idx):
    return np.asarray(idx).reshape(8, -1, 16).transpose(0, 2, 1).reshape(128, -1).astype(np.uint16)


def unstriped8(offs):
    return offs.reshape(8, 16, -1).transpose(0, 2, 1).reshape(8, -1).astype(np.int64)


def pick8(x, idx, run):
    r = np.arange(len(x))
    return x[r[:, None], idx[r % (8 * run) // run]]


E2M1 = np.array([0.0, 0.5, 1.0, 1.5, 2.0, 3.0, 4.0, 6.0, -0.0, -0.5, -1.0, -1.5, -2.0, -3.0, -4.0, -6.0])


def pack_weight(w, fmt):
    k, n = w.shape
    w = f64(np.asarray(w, np.float32).astype(ml_dtypes.bfloat16)).reshape(k // 32, 32, n)
    amax = np.abs(w).max(1)
    if fmt == "e4m3":
        byte = np.frexp(amax)[1] - 1 + 127 - 7
    else:
        mant, ex = np.frexp(amax / 6.0)
        byte = np.where(mant > 0.5, ex, ex - 1) + 127
    byte = np.clip(np.where(amax > 0, byte, 1), 1, 254)
    scaled = (w * np.exp2(127.0 - byte)[:, None, :]).reshape(k, n).astype(np.float32)
    by_word = np.ascontiguousarray(scaled.reshape(k // 512, 128, 4, n).transpose(0, 1, 3, 2))
    if fmt == "e4m3":
        words = by_word.astype(ml_dtypes.float8_e4m3fn).view(np.uint8)
    else:
        c = by_word.astype(ml_dtypes.float4_e2m1fn).view(np.uint8) & 0xF
        words = (c[..., 0::2] | (c[..., 1::2] << 4)).reshape(k // 512, 128, 2 * n)
    return np.ascontiguousarray(words), np.ascontiguousarray(byte.astype(np.uint8).reshape(k // 512, 16, n))


def unpack_weight(words, scales, fmt):
    g, _, n = scales.shape
    words = np.ascontiguousarray(words).reshape(g, 128, n, -1)
    if fmt == "e4m3":
        vals = words.view(ml_dtypes.float8_e4m3fn).astype(np.float64)
    else:
        nib = np.empty((g, 128, n, 4), np.uint8)
        nib[..., 0::2] = words & 0xF
        nib[..., 1::2] = words >> 4
        vals = E2M1[nib]
    vals = vals * np.repeat(np.exp2(scales.astype(np.float64) - 127.0), 8, axis=1)[..., None]
    return vals.transpose(0, 1, 3, 2).reshape(g * 512, n)


D, K, T, U, I, Q = 512, 512, 1024, 1024, 512, 128


def setup_inputs():
    n = np.random.standard_normal
    idx = np.stack([np.random.permutation(T)[:I] for _ in range(8)])
    idx2 = np.stack([np.random.permutation(U)[:I] for _ in range(8)])
    idx3 = np.stack([np.random.permutation(T)[:I] for _ in range(8)])
    idx4 = np.stack([np.random.permutation(U)[:I] for _ in range(8)])
    fd = mx_kscale(D)
    fk = mx_kscale(K)
    wqp = pack_weight(n((D, K)) * 1.0 / np.sqrt(D) * fd[:, None] * fk, "e4m3")
    keysp = pack_weight(n((K, T)) * 1.0 / np.sqrt(K) / fk[:, None], "e4m3")
    notesp = pack_weight(n((K, U)) * 1.0 / np.sqrt(K) / fk[:, None], "e2m1")
    return {
        "states": (n((D, Q)) * 0.95 / fd[:, None]).astype(np.float32),
        "wq_words": wqp[0],
        "wq_scales": wqp[1],
        "keys_words": keysp[0],
        "keys_scales": keysp[1],
        "notes_words": notesp[0],
        "notes_scales": notesp[1],
        "lam": (np.random.uniform(0.5, 1.5, (Q, 1))).astype(np.float32),
        "offs": striped8(idx),
        "offs2": striped8(idx2),
        "offs3": striped8(idx3),
        "offs4": striped8(idx4),
    }


def reference(states, wq_words, wq_scales, keys_words, keys_scales, notes_words, notes_scales, lam, offs, offs2, offs3, offs4):
    idx = unstriped8(offs)
    idx2 = unstriped8(offs2)
    idx3 = unstriped8(offs3)
    idx4 = unstriped8(offs4)
    wqu = unpack_weight(wq_words, wq_scales, "e4m3")
    keysu = unpack_weight(keys_words, keys_scales, "e4m3")
    notesu = unpack_weight(notes_words, notes_scales, "e2m1")
    statesq = mxq(f64(states), 0, "e4m3")
    qv = wqu.T @ statesq
    qvq = mxq(qv, 0, "e4m3")
    a = qvq.T @ keysu
    b = qvq.T @ notesu
    r = pick8(b, idx2, 16) - pick8(a, idx, 16)
    f1 = np.zeros((Q, T))
    f1[np.arange(Q)[:, None], idx[np.arange(Q) % 128 // 16]] = r
    f2 = np.zeros((Q, U))
    f2[np.arange(Q)[:, None], idx2[np.arange(Q) % 128 // 16]] = r
    a2 = a + f1
    b2 = b - f2
    y = pick8(a2, idx3, 16) - pick8(b2, idx4, 16) * f64(lam)
    return y

@@ -1,0 +1,187 @@
+from contextlib import ExitStack
+
+import concourse.mybir as mybir
+
+F32 = mybir.dt.float32
+BF16 = mybir.dt.bfloat16
+I32 = mybir.dt.int32
+U32 = mybir.dt.uint32
+U16 = mybir.dt.uint16
+U8 = mybir.dt.uint8
+FP8X4 = mybir.dt.float8_e4m3fn_x4
+FP4X4 = mybir.dt.float4_e2m1fn_x4
+ADD = mybir.AluOpType.add
+SUB = mybir.AluOpType.subtract
+MULT = mybir.AluOpType.mult
+COPY = mybir.ActivationFunctionType.Copy
+
+P = 128
+PACK = 4
+D, K, T, U, SLOTS, Q = 512, 512, 1024, 1024, 512, 128
+BANK = 512
+B_PIECE = 256
+A2_SPLIT = 768
+HALF = SLOTS // 2
+LIST_COLS = SLOTS // 16
+FLOPS = 2 * D * K * Q + 2 * K * Q * T + 2 * K * Q * U
+
+
+def load_scale_rows(queue, plane, scales):
+    for quad in range(4):
+        queue.dma_start(
+            out=plane[32 * quad : 32 * quad + 4, :].bitcast(I32),
+            in_=scales[0][4 * quad : 4 * quad + 4, :].bitcast(I32),
+        )
+
+
+def tile_attend_traded_madetwo_kernel(
+    tc, states, wq_words, wq_scales, keys_words, keys_scales, notes_words, notes_scales, lam, offs, offs2, offs3, offs4, out
+):
+    nc = tc.nc
+    with ExitStack() as ctx:
+        sb = ctx.enter_context(tc.tile_pool(name="sb", bufs=1))
+        ps = ctx.enter_context(tc.psum_pool(name="ps", bufs=1))
+
+        wq_plane_raw = sb.tile([P, K], U8, align_bytes=64)
+        nc.vector.memset(wq_plane_raw[:].bitcast(I32), 0)
+        load_scale_rows(nc.sync, wq_plane_raw, wq_scales)
+
+        states_raw = sb.tile([P, PACK, Q], F32, align_bytes=64)
+        nc.sync.dma_start(out=states_raw[:], in_=states.rearrange("(p j) q -> p j q", j=PACK))
+        wq_raw = sb.tile([P, K], U32, align_bytes=64)
+        nc.sync.dma_start(out=wq_raw[:].bitcast(I32), in_=wq_words[0].rearrange("p n t -> p (n t)").bitcast(I32))
+        keys = sb.tile([P, T], U32, align_bytes=64)
+        nc.sync.dma_start(out=keys[:].bitcast(I32), in_=keys_words[0].rearrange("p n t -> p (n t)").bitcast(I32))
+        notes = sb.tile([P, 2 * U], U8, align_bytes=64)
+        nc.sync.dma_start(out=notes[:].bitcast(I32), in_=notes_words[0].bitcast(I32))
+        keys_plane = sb.tile([P, T], U8, align_bytes=64)
+        load_scale_rows(nc.sync, keys_plane, keys_scales)
+        notes_plane = sb.tile([P, U], U8, align_bytes=64)
+        load_scale_rows(nc.sync, notes_plane, notes_scales)
+        list1 = sb.tile([P, LIST_COLS], U16)
+        nc.sync.dma_start(list1[:], offs)
+        list2 = sb.tile([P, LIST_COLS], U16)
+        nc.sync.dma_start(list2[:], offs2)
+        list4 = sb.tile([P, LIST_COLS], U16)
+        nc.sync.dma_start(list4[:], offs4)
+        lam_col = sb.tile([P, 1], F32)
+        nc.sync.dma_start(out=lam_col[:], in_=lam)
+        list3 = sb.tile([P, LIST_COLS], U16)
+        nc.sync.dma_start(list3[:], offs3)
+
+        f1 = sb.tile([P, T], F32)
+        nc.vector.memset(f1[:], 0.0)
+        f2 = sb.tile([P, U], F32)
+        nc.vector.memset(f2[:], 0.0)
+
+        wq_plane = sb.tile([P, PACK, P], U8, align_bytes=64)
+        nc.vector.tensor_copy(
+            out=wq_plane[:].rearrange("p t m -> p m t"), in_=wq_plane_raw[:].rearrange("p (m t) -> p m t", t=PACK)
+        )
+        wq_dealt = sb.tile([P, PACK, P], U32, align_bytes=64)
+        nc.scalar.copy(out=wq_dealt[:].rearrange("p t m -> p m t"), in_=wq_raw[:].rearrange("p (m t) -> p m t", t=PACK))
+
+        states_bf = sb.tile([P, Q, PACK], BF16, align_bytes=64)
+        nc.vector.tensor_copy(out=states_bf[:], in_=states_raw[:].rearrange("p j q -> p q j"))
+        states_codes = sb.tile([P, Q], U32, align_bytes=64)
+        states_plane = sb.tile([P, Q], U8, align_bytes=64)
+        nc.vector.quantize_mx(
+            out=states_codes[:].bitcast(FP8X4), scales=states_plane[:], in_=states_bf[:].rearrange("p q j -> p (q j)")
+        )
+
+        qv_ps = ps.tile([P, PACK, Q], F32)
+        for t in range(PACK):
+            nc.tensor.matmul_mx(
+                out=qv_ps[:, t, :],
+                lhsT=wq_dealt[:, t, :].bitcast(FP8X4),
+                lhsT_scale=wq_plane[:, t, :],
+                rhs=states_codes[:].bitcast(FP8X4),
+                rhs_scale=states_plane[:],
+                start=True,
+                stop=True,
+            )
+        qv_bf = sb.tile([P, Q, PACK], BF16, align_bytes=64)
+        nc.scalar.copy(out=qv_bf[:], in_=qv_ps[:].rearrange("p t q -> p q t"))
+        qv_codes = sb.tile([P, Q], U32, align_bytes=64)
+        qv_plane = sb.tile([P, Q], U8, align_bytes=64)
+        nc.vector.quantize_mx(
+            out=qv_codes[:].bitcast(FP8X4), scales=qv_plane[:], in_=qv_bf[:].rearrange("p q t -> p (q t)")
+        )
+
+        a = sb.tile([P, T], F32)
+        b = sb.tile([P, U], F32)
+        a_banks = []
+        for h in range(T // BANK):
+            cols = slice(h * BANK, (h + 1) * BANK)
+            a_ps = ps.tile([P, BANK], F32, name="a_ps%d" % h)
+            a_banks.append(a_ps)
+            nc.tensor.matmul_mx(
+                out=a_ps[:],
+                lhsT=qv_codes[:].bitcast(FP8X4),
+                lhsT_scale=qv_plane[:],
+                rhs=keys[:, cols].bitcast(FP8X4),
+                rhs_scale=keys_plane[:, cols],
+                start=True,
+                stop=True,
+            )
+            if h == 0:
+                nc.scalar.copy(out=a[:, cols], in_=a_ps[:])
+            else:
+                nc.vector.tensor_copy(out=a[:, cols], in_=a_ps[:])
+        for h in range(U // B_PIECE):
+            cols = slice(h * B_PIECE, (h + 1) * B_PIECE)
+            b_ps = ps.tile([P, B_PIECE], F32, name="b_ps%d" % h)
+            nc.tensor.matmul_mx(
+                out=b_ps[:],
+                lhsT=qv_codes[:].bitcast(FP8X4),
+                lhsT_scale=qv_plane[:],
+                rhs=notes[:, 2 * h * B_PIECE : 2 * (h + 1) * B_PIECE].bitcast(FP4X4),
+                rhs_scale=notes_plane[:, cols],
+                start=True,
+                stop=True,
+            )
+            if h == 0:
+                nc.scalar.copy(out=b[:, cols], in_=b_ps[:])
+            else:
+                nc.vector.tensor_copy(out=b[:, cols], in_=b_ps[:])
+
+        first = slice(0, HALF)
+        second = slice(HALF, SLOTS)
+        first_cols = slice(0, LIST_COLS // 2)
+        second_cols = slice(LIST_COLS // 2, LIST_COLS)
+
+        neg_lam = sb.tile([P, 1], F32)
+        nc.gpsimd.tensor_scalar(neg_lam[:], lam_col[:], -1.0, None, MULT)
+
+        a_listed = sb.tile([P, SLOTS], F32)
+        nc.scalar.activation(a_listed[:, first], a[:].indirect(list1[:, first_cols]), COPY)
+        r = sb.tile([P, SLOTS], F32)
+        nc.vector.tensor_tensor(r[:, first], b[:].indirect(list2[:, first_cols]), a_listed[:, first], SUB)
+        nc.scalar.activation(a_listed[:, second], a[:].indirect(list1[:, second_cols]), COPY)
+        b_listed = sb.tile([P, HALF], F32)
+        nc.scalar.activation(b_listed[:], b[:].indirect(list2[:, second_cols]), COPY)
+        nc.gpsimd.tensor_tensor(r[:, second], b_listed[:], a_listed[:, second], SUB)
+
+        nc.vector.tensor_copy(f2[:].indirect(list2[:, first_cols]), r[:, first])
+        nc.vector.tensor_copy(f2[:].indirect(list2[:, second_cols]), r[:, second])
+        nc.vector.tensor_copy(f1[:].indirect(list1[:]), r[:])
+
+        b2 = sb.tile([P, U], F32)
+        nc.gpsimd.tensor_tensor(b2[:], b[:], f2[:], SUB)
+        b2_listed = sb.tile([P, SLOTS], F32)
+        nc.scalar.activation(b2_listed[:, first], b2[:].indirect(list4[:, first_cols]), COPY)
+        weighted = sb.tile([P, HALF], F32)
+        nc.scalar.activation(weighted[:], b2_listed[:, first], COPY, scale=neg_lam[:])
+        nc.scalar.activation(b2_listed[:, second], b2[:].indirect(list4[:, second_cols]), COPY)
+
+        a2 = sb.tile([P, T], F32)
+        nc.gpsimd.tensor_tensor(a2[:, A2_SPLIT:T], a[:, A2_SPLIT:T], f1[:, A2_SPLIT:T], ADD)
+        nc.vector.tensor_tensor(a2[:, 0:BANK], a_banks[0][:], f1[:, 0:BANK], ADD)
+        nc.vector.tensor_tensor(a2[:, BANK:A2_SPLIT], a_banks[1][:, 0 : A2_SPLIT - BANK], f1[:, BANK:A2_SPLIT], ADD)
+        result = sb.tile([P, SLOTS], F32)
+        nc.vector.tensor_tensor(result[:, first], a2[:].indirect(list3[:, first_cols]), weighted[:], ADD)
+        nc.sync.dma_start(out=out[:, first], in_=result[:, first])
+        a2_listed = sb.tile([P, HALF], F32)
+        nc.scalar.activation(a2_listed[:], a2[:].indirect(list3[:, second_cols]), COPY)
+        nc.vector.scalar_tensor_tensor(result[:, second], b2_listed[:, second], neg_lam[:], a2_listed[:], MULT, ADD)
+        nc.sync.dma_start(out=out[:, second], in_=result[:, second])

@@ -20,6 +20,7 @@ PACK = 4
 D, K, T, U, SLOTS, Q = 512, 512, 1024, 1024, 512, 128
 BANK = 512
 B_PIECE = 256
+CAST_SPLIT = 64
 A2_SPLIT = 768
 HALF = SLOTS // 2
 LIST_COLS = SLOTS // 16
@@ -74,26 +75,30 @@ def tile_attend_traded_madetwo_kernel(
         f2 = sb.tile([P, U], F32)
         nc.vector.memset(f2[:], 0.0)
 
+        states_bf = sb.tile([P, Q, PACK], BF16, align_bytes=64)
+        states_by_row = states_raw[:].rearrange("p j q -> p q j")
+        nc.vector.tensor_copy(out=states_bf[:, 0:CAST_SPLIT, :], in_=states_by_row[:, 0:CAST_SPLIT, :])
+        nc.scalar.copy(out=states_bf[:, CAST_SPLIT:Q, :], in_=states_by_row[:, CAST_SPLIT:Q, :])
         wq_plane = sb.tile([P, PACK, P], U8, align_bytes=64)
         nc.vector.tensor_copy(
             out=wq_plane[:].rearrange("p t m -> p m t"), in_=wq_plane_raw[:].rearrange("p (m t) -> p m t", t=PACK)
         )
-        wq_dealt = sb.tile([P, PACK, P], U32, align_bytes=64)
-        nc.scalar.copy(out=wq_dealt[:].rearrange("p t m -> p m t"), in_=wq_raw[:].rearrange("p (m t) -> p m t", t=PACK))
-
-        states_bf = sb.tile([P, Q, PACK], BF16, align_bytes=64)
-        nc.vector.tensor_copy(out=states_bf[:], in_=states_raw[:].rearrange("p j q -> p q j"))
         states_codes = sb.tile([P, Q], U32, align_bytes=64)
         states_plane = sb.tile([P, Q], U8, align_bytes=64)
         nc.vector.quantize_mx(
             out=states_codes[:].bitcast(FP8X4), scales=states_plane[:], in_=states_bf[:].rearrange("p q j -> p (q j)")
         )
+        wq_by_place = wq_raw[:].rearrange("p (m t) -> p m t", t=PACK)
+        wq_low = sb.tile([P, 2, P], U32, align_bytes=64)
+        nc.scalar.copy(out=wq_low[:].rearrange("p t m -> p m t"), in_=wq_by_place[:, :, 0:2])
+        wq_high = sb.tile([P, 2, P], U32, align_bytes=64)
+        nc.vector.tensor_copy(out=wq_high[:].rearrange("p t m -> p m t"), in_=wq_by_place[:, :, 2:4])
 
         qv_ps = ps.tile([P, PACK, Q], F32)
         for t in range(PACK):
             nc.tensor.matmul_mx(
                 out=qv_ps[:, t, :],
-                lhsT=wq_dealt[:, t, :].bitcast(FP8X4),
+                lhsT=(wq_low, wq_high)[t // 2][:, t % 2, :].bitcast(FP8X4),
                 lhsT_scale=wq_plane[:, t, :],
                 rhs=states_codes[:].bitcast(FP8X4),
                 rhs_scale=states_plane[:],
@@ -111,23 +116,22 @@ def tile_attend_traded_madetwo_kernel(
         a = sb.tile([P, T], F32)
         b = sb.tile([P, U], F32)
         a_banks = []
-        for h in range(T // BANK):
-            cols = slice(h * BANK, (h + 1) * BANK)
-            a_ps = ps.tile([P, BANK], F32, name="a_ps%d" % h)
+        for h, (lo, hi) in enumerate(((0, 512), (512, 768), (768, 1024))):
+            a_ps = ps.tile([P, hi - lo], F32, name="a_ps%d" % h)
             a_banks.append(a_ps)
             nc.tensor.matmul_mx(
                 out=a_ps[:],
                 lhsT=qv_codes[:].bitcast(FP8X4),
                 lhsT_scale=qv_plane[:],
-                rhs=keys[:, cols].bitcast(FP8X4),
-                rhs_scale=keys_plane[:, cols],
+                rhs=keys[:, lo:hi].bitcast(FP8X4),
+                rhs_scale=keys_plane[:, lo:hi],
                 start=True,
                 stop=True,
             )
             if h == 0:
-                nc.scalar.copy(out=a[:, cols], in_=a_ps[:])
+                nc.scalar.copy(out=a[:, lo:hi], in_=a_ps[:])
             else:
-                nc.vector.tensor_copy(out=a[:, cols], in_=a_ps[:])
+                nc.vector.tensor_copy(out=a[:, lo:hi], in_=a_ps[:])
         for h in range(U // B_PIECE):
             cols = slice(h * B_PIECE, (h + 1) * B_PIECE)
             b_ps = ps.tile([P, B_PIECE], F32, name="b_ps%d" % h)
@@ -150,21 +154,21 @@ def tile_attend_traded_madetwo_kernel(
         first_cols = slice(0, LIST_COLS // 2)
         second_cols = slice(LIST_COLS // 2, LIST_COLS)
 
+        a_first = sb.tile([P, HALF], F32)
+        nc.scalar.activation(a_first[:], a[:].indirect(list1[:, first_cols]), COPY)
+        neg_a_second = sb.tile([P, HALF], F32)
+        nc.scalar.activation(neg_a_second[:], a[:].indirect(list1[:, second_cols]), COPY, scale=-1.0)
+        r = sb.tile([P, SLOTS], F32)
+        nc.vector.tensor_tensor(r[:, first], b[:].indirect(list2[:, first_cols]), a_first[:], SUB)
+        nc.scalar.activation(r[:, second], b[:].indirect(list2[:, second_cols]), COPY)
+
+        nc.vector.tensor_tensor(f2[:].indirect(list2[:, second_cols]), r[:, second], neg_a_second[:], ADD)
+        nc.gpsimd.tensor_tensor(r[:, second], r[:, second], neg_a_second[:], ADD)
+        nc.vector.tensor_copy(f2[:].indirect(list2[:, first_cols]), r[:, first])
+        nc.vector.tensor_copy(f1[:].indirect(list1[:]), r[:])
+
         neg_lam = sb.tile([P, 1], F32)
         nc.gpsimd.tensor_scalar(neg_lam[:], lam_col[:], -1.0, None, MULT)
-
-        a_listed = sb.tile([P, SLOTS], F32)
-        nc.scalar.activation(a_listed[:, first], a[:].indirect(list1[:, first_cols]), COPY)
-        r = sb.tile([P, SLOTS], F32)
-        nc.vector.tensor_tensor(r[:, first], b[:].indirect(list2[:, first_cols]), a_listed[:, first], SUB)
-        nc.scalar.activation(a_listed[:, second], a[:].indirect(list1[:, second_cols]), COPY)
-        b_listed = sb.tile([P, HALF], F32)
-        nc.scalar.activation(b_listed[:], b[:].indirect(list2[:, second_cols]), COPY)
-        nc.gpsimd.tensor_tensor(r[:, second], b_listed[:], a_listed[:, second], SUB)
-
-        nc.vector.tensor_copy(f2[:].indirect(list2[:, first_cols]), r[:, first])
-        nc.vector.tensor_copy(f2[:].indirect(list2[:, second_cols]), r[:, second])
-        nc.vector.tensor_copy(f1[:].indirect(list1[:]), r[:])
 
         b2 = sb.tile([P, U], F32)
         nc.gpsimd.tensor_tensor(b2[:], b[:], f2[:], SUB)

@@ -17,19 +17,20 @@ COPY = mybir.ActivationFunctionType.Copy
 
 P = 128
 PACK = 4
+QUADS = 4
 D, K, T, U, SLOTS, Q = 512, 512, 1024, 1024, 512, 128
-BANK = 512
-B_PIECE = 256
-CAST_SPLIT = 64
-A2_SPLIT = 768
 HALF = SLOTS // 2
 LIST_COLS = SLOTS // 16
+CAST_SPLIT = 64
+A_PIECES = ((0, 512), (512, 768), (768, 896), (896, 1024))
+B_PIECE = 256
+A2_SPLIT = 704
 FLOPS = 2 * D * K * Q + 2 * K * Q * T + 2 * K * Q * U
 
 
-def load_scale_rows(queue, plane, scales):
-    for quad in range(4):
-        queue.dma_start(
+def load_scale_rows(nc, plane, scales, quads):
+    for quad in quads:
+        nc.sync.dma_start(
             out=plane[32 * quad : 32 * quad + 4, :].bitcast(I32),
             in_=scales[0][4 * quad : 4 * quad + 4, :].bitcast(I32),
         )
@@ -45,7 +46,7 @@ def tile_attend_traded_madetwo_kernel(
 
         wq_plane_raw = sb.tile([P, K], U8, align_bytes=64)
         nc.vector.memset(wq_plane_raw[:].bitcast(I32), 0)
-        load_scale_rows(nc.sync, wq_plane_raw, wq_scales)
+        load_scale_rows(nc, wq_plane_raw, wq_scales, range(QUADS))
 
         states_raw = sb.tile([P, PACK, Q], F32, align_bytes=64)
         nc.sync.dma_start(out=states_raw[:], in_=states.rearrange("(p j) q -> p j q", j=PACK))
@@ -53,12 +54,13 @@ def tile_attend_traded_madetwo_kernel(
         nc.sync.dma_start(out=wq_raw[:].bitcast(I32), in_=wq_words[0].rearrange("p n t -> p (n t)").bitcast(I32))
         keys = sb.tile([P, T], U32, align_bytes=64)
         nc.sync.dma_start(out=keys[:].bitcast(I32), in_=keys_words[0].rearrange("p n t -> p (n t)").bitcast(I32))
+        notes_plane = sb.tile([P, U], U8, align_bytes=64)
+        load_scale_rows(nc, notes_plane, notes_scales, range(1))
         notes = sb.tile([P, 2 * U], U8, align_bytes=64)
         nc.sync.dma_start(out=notes[:].bitcast(I32), in_=notes_words[0].bitcast(I32))
         keys_plane = sb.tile([P, T], U8, align_bytes=64)
-        load_scale_rows(nc.sync, keys_plane, keys_scales)
-        notes_plane = sb.tile([P, U], U8, align_bytes=64)
-        load_scale_rows(nc.sync, notes_plane, notes_scales)
+        load_scale_rows(nc, keys_plane, keys_scales, range(QUADS))
+        load_scale_rows(nc, notes_plane, notes_scales, range(1, QUADS))
         list1 = sb.tile([P, LIST_COLS], U16)
         nc.sync.dma_start(list1[:], offs)
         list2 = sb.tile([P, LIST_COLS], U16)
@@ -88,17 +90,18 @@ def tile_attend_traded_madetwo_kernel(
         nc.vector.quantize_mx(
             out=states_codes[:].bitcast(FP8X4), scales=states_plane[:], in_=states_bf[:].rearrange("p q j -> p (q j)")
         )
-        wq_by_place = wq_raw[:].rearrange("p (m t) -> p m t", t=PACK)
-        wq_low = sb.tile([P, 2, P], U32, align_bytes=64)
-        nc.scalar.copy(out=wq_low[:].rearrange("p t m -> p m t"), in_=wq_by_place[:, :, 0:2])
-        wq_high = sb.tile([P, 2, P], U32, align_bytes=64)
-        nc.vector.tensor_copy(out=wq_high[:].rearrange("p t m -> p m t"), in_=wq_by_place[:, :, 2:4])
+        wq_by_group = wq_raw[:].rearrange("p (m t) -> p m t", t=PACK)
+        wq_group0 = sb.tile([P, 1, P], U32, align_bytes=64)
+        nc.scalar.copy(out=wq_group0[:].rearrange("p t m -> p m t"), in_=wq_by_group[:, :, 0:1])
+        wq_later_groups = sb.tile([P, PACK - 1, P], U32, align_bytes=64)
+        nc.vector.tensor_copy(out=wq_later_groups[:].rearrange("p t m -> p m t"), in_=wq_by_group[:, :, 1:PACK])
 
-        qv_ps = ps.tile([P, PACK, Q], F32)
+        qv_low = ps.tile([P, 2, Q], F32, tag="bank0")
+        qv_high = ps.tile([P, 2, Q], F32, tag="bank1")
         for t in range(PACK):
             nc.tensor.matmul_mx(
-                out=qv_ps[:, t, :],
-                lhsT=(wq_low, wq_high)[t // 2][:, t % 2, :].bitcast(FP8X4),
+                out=(qv_low, qv_high)[t // 2][:, t % 2, :],
+                lhsT=(wq_group0[:, 0, :] if t == 0 else wq_later_groups[:, t - 1, :]).bitcast(FP8X4),
                 lhsT_scale=wq_plane[:, t, :],
                 rhs=states_codes[:].bitcast(FP8X4),
                 rhs_scale=states_plane[:],
@@ -106,7 +109,8 @@ def tile_attend_traded_madetwo_kernel(
                 stop=True,
             )
         qv_bf = sb.tile([P, Q, PACK], BF16, align_bytes=64)
-        nc.scalar.copy(out=qv_bf[:], in_=qv_ps[:].rearrange("p t q -> p q t"))
+        nc.vector.tensor_copy(out=qv_bf[:, :, 0:2], in_=qv_low[:].rearrange("p t q -> p q t"))
+        nc.scalar.copy(out=qv_bf[:, :, 2:PACK], in_=qv_high[:].rearrange("p t q -> p q t"))
         qv_codes = sb.tile([P, Q], U32, align_bytes=64)
         qv_plane = sb.tile([P, Q], U8, align_bytes=64)
         nc.vector.quantize_mx(
@@ -116,8 +120,8 @@ def tile_attend_traded_madetwo_kernel(
         a = sb.tile([P, T], F32)
         b = sb.tile([P, U], F32)
         a_banks = []
-        for h, (lo, hi) in enumerate(((0, 512), (512, 768), (768, 1024))):
-            a_ps = ps.tile([P, hi - lo], F32, name="a_ps%d" % h)
+        for piece, (lo, hi) in enumerate(A_PIECES):
+            a_ps = ps.tile([P, hi - lo], F32, name="a_ps%d" % piece, tag="bank%d" % piece)
             a_banks.append(a_ps)
             nc.tensor.matmul_mx(
                 out=a_ps[:],
@@ -128,26 +132,23 @@ def tile_attend_traded_madetwo_kernel(
                 start=True,
                 stop=True,
             )
-            if h == 0:
+            if piece in (0, len(A_PIECES) - 1):
                 nc.scalar.copy(out=a[:, lo:hi], in_=a_ps[:])
             else:
                 nc.vector.tensor_copy(out=a[:, lo:hi], in_=a_ps[:])
-        for h in range(U // B_PIECE):
-            cols = slice(h * B_PIECE, (h + 1) * B_PIECE)
-            b_ps = ps.tile([P, B_PIECE], F32, name="b_ps%d" % h)
+        for piece in range(U // B_PIECE):
+            cols = slice(piece * B_PIECE, (piece + 1) * B_PIECE)
+            b_ps = ps.tile([P, B_PIECE], F32, name="b_ps%d" % piece)
             nc.tensor.matmul_mx(
                 out=b_ps[:],
                 lhsT=qv_codes[:].bitcast(FP8X4),
                 lhsT_scale=qv_plane[:],
-                rhs=notes[:, 2 * h * B_PIECE : 2 * (h + 1) * B_PIECE].bitcast(FP4X4),
+                rhs=notes[:, 2 * piece * B_PIECE : 2 * (piece + 1) * B_PIECE].bitcast(FP4X4),
                 rhs_scale=notes_plane[:, cols],
                 start=True,
                 stop=True,
             )
-            if h == 0:
-                nc.scalar.copy(out=b[:, cols], in_=b_ps[:])
-            else:
-                nc.vector.tensor_copy(out=b[:, cols], in_=b_ps[:])
+            nc.vector.tensor_copy(out=b[:, cols], in_=b_ps[:])
 
         first = slice(0, HALF)
         second = slice(HALF, SLOTS)
@@ -174,18 +175,22 @@ def tile_attend_traded_madetwo_kernel(
         nc.gpsimd.tensor_tensor(b2[:], b[:], f2[:], SUB)
         b2_listed = sb.tile([P, SLOTS], F32)
         nc.scalar.activation(b2_listed[:, first], b2[:].indirect(list4[:, first_cols]), COPY)
-        weighted = sb.tile([P, HALF], F32)
-        nc.scalar.activation(weighted[:], b2_listed[:, first], COPY, scale=neg_lam[:])
+        weighted_first = sb.tile([P, HALF], F32)
+        nc.scalar.activation(weighted_first[:], b2_listed[:, first], COPY, scale=neg_lam[:])
         nc.scalar.activation(b2_listed[:, second], b2[:].indirect(list4[:, second_cols]), COPY)
 
         a2 = sb.tile([P, T], F32)
+        bank1_start = A_PIECES[1][0]
         nc.gpsimd.tensor_tensor(a2[:, A2_SPLIT:T], a[:, A2_SPLIT:T], f1[:, A2_SPLIT:T], ADD)
-        nc.vector.tensor_tensor(a2[:, 0:BANK], a_banks[0][:], f1[:, 0:BANK], ADD)
-        nc.vector.tensor_tensor(a2[:, BANK:A2_SPLIT], a_banks[1][:, 0 : A2_SPLIT - BANK], f1[:, BANK:A2_SPLIT], ADD)
+        nc.vector.tensor_tensor(a2[:, 0:bank1_start], a_banks[0][:], f1[:, 0:bank1_start], ADD)
+        nc.vector.tensor_tensor(
+            a2[:, bank1_start:A2_SPLIT], a_banks[1][:, 0 : A2_SPLIT - bank1_start], f1[:, bank1_start:A2_SPLIT], ADD
+        )
+
         result = sb.tile([P, SLOTS], F32)
-        nc.vector.tensor_tensor(result[:, first], a2[:].indirect(list3[:, first_cols]), weighted[:], ADD)
+        nc.vector.tensor_tensor(result[:, first], a2[:].indirect(list3[:, first_cols]), weighted_first[:], ADD)
         nc.sync.dma_start(out=out[:, first], in_=result[:, first])
-        a2_listed = sb.tile([P, HALF], F32)
-        nc.scalar.activation(a2_listed[:], a2[:].indirect(list3[:, second_cols]), COPY)
-        nc.vector.scalar_tensor_tensor(result[:, second], b2_listed[:, second], neg_lam[:], a2_listed[:], MULT, ADD)
+        a2_second = sb.tile([P, HALF], F32)
+        nc.scalar.activation(a2_second[:], a2[:].indirect(list3[:, second_cols]), COPY)
+        nc.vector.scalar_tensor_tensor(result[:, second], b2_listed[:, second], neg_lam[:], a2_second[:], MULT, ADD)
         nc.sync.dma_start(out=out[:, second], in_=result[:, second])

from contextlib import ExitStack

import concourse.mybir as mybir

F32 = mybir.dt.float32
BF16 = mybir.dt.bfloat16
I32 = mybir.dt.int32
U32 = mybir.dt.uint32
U16 = mybir.dt.uint16
U8 = mybir.dt.uint8
FP8X4 = mybir.dt.float8_e4m3fn_x4
FP4X4 = mybir.dt.float4_e2m1fn_x4
ADD = mybir.AluOpType.add
SUB = mybir.AluOpType.subtract
MULT = mybir.AluOpType.mult
COPY = mybir.ActivationFunctionType.Copy

P = 128
PACK = 4
QUADS = 4
D, K, T, U, SLOTS, Q = 512, 512, 1024, 1024, 512, 128
HALF = SLOTS // 2
LIST_COLS = SLOTS // 16
CAST_SPLIT = 64
A_PIECES = ((0, 512), (512, 768), (768, 896), (896, 1024))
B_PIECE = 256
A2_SPLIT = 704
FLOPS = 2 * D * K * Q + 2 * K * Q * T + 2 * K * Q * U


def load_scale_rows(nc, plane, scales, quads):
    for quad in quads:
        nc.sync.dma_start(
            out=plane[32 * quad : 32 * quad + 4, :].bitcast(I32),
            in_=scales[0][4 * quad : 4 * quad + 4, :].bitcast(I32),
        )


def tile_attend_traded_madetwo_kernel(
    tc, states, wq_words, wq_scales, keys_words, keys_scales, notes_words, notes_scales, lam, offs, offs2, offs3, offs4, out
):
    nc = tc.nc
    with ExitStack() as ctx:
        sb = ctx.enter_context(tc.tile_pool(name="sb", bufs=1))
        ps = ctx.enter_context(tc.psum_pool(name="ps", bufs=1))

        wq_plane_raw = sb.tile([P, K], U8, align_bytes=64)
        nc.vector.memset(wq_plane_raw[:].bitcast(I32), 0)
        load_scale_rows(nc, wq_plane_raw, wq_scales, range(QUADS))

        states_raw = sb.tile([P, PACK, Q], F32, align_bytes=64)
        nc.sync.dma_start(out=states_raw[:], in_=states.rearrange("(p j) q -> p j q", j=PACK))
        wq_raw = sb.tile([P, K], U32, align_bytes=64)
        nc.sync.dma_start(out=wq_raw[:].bitcast(I32), in_=wq_words[0].rearrange("p n t -> p (n t)").bitcast(I32))
        keys = sb.tile([P, T], U32, align_bytes=64)
        nc.sync.dma_start(out=keys[:].bitcast(I32), in_=keys_words[0].rearrange("p n t -> p (n t)").bitcast(I32))
        notes_plane = sb.tile([P, U], U8, align_bytes=64)
        load_scale_rows(nc, notes_plane, notes_scales, range(1))
        notes = sb.tile([P, 2 * U], U8, align_bytes=64)
        nc.sync.dma_start(out=notes[:].bitcast(I32), in_=notes_words[0].bitcast(I32))
        keys_plane = sb.tile([P, T], U8, align_bytes=64)
        load_scale_rows(nc, keys_plane, keys_scales, range(QUADS))
        load_scale_rows(nc, notes_plane, notes_scales, range(1, QUADS))
        list1 = sb.tile([P, LIST_COLS], U16)
        nc.sync.dma_start(list1[:], offs)
        list2 = sb.tile([P, LIST_COLS], U16)
        nc.sync.dma_start(list2[:], offs2)
        list4 = sb.tile([P, LIST_COLS], U16)
        nc.sync.dma_start(list4[:], offs4)
        lam_col = sb.tile([P, 1], F32)
        nc.sync.dma_start(out=lam_col[:], in_=lam)
        list3 = sb.tile([P, LIST_COLS], U16)
        nc.sync.dma_start(list3[:], offs3)

        f1 = sb.tile([P, T], F32)
        nc.vector.memset(f1[:], 0.0)
        f2 = sb.tile([P, U], F32)
        nc.vector.memset(f2[:], 0.0)

        states_bf = sb.tile([P, Q, PACK], BF16, align_bytes=64)
        states_by_row = states_raw[:].rearrange("p j q -> p q j")
        nc.vector.tensor_copy(out=states_bf[:, 0:CAST_SPLIT, :], in_=states_by_row[:, 0:CAST_SPLIT, :])
        nc.scalar.copy(out=states_bf[:, CAST_SPLIT:Q, :], in_=states_by_row[:, CAST_SPLIT:Q, :])
        wq_plane = sb.tile([P, PACK, P], U8, align_bytes=64)
        nc.vector.tensor_copy(
            out=wq_plane[:].rearrange("p t m -> p m t"), in_=wq_plane_raw[:].rearrange("p (m t) -> p m t", t=PACK)
        )
        states_codes = sb.tile([P, Q], U32, align_bytes=64)
        states_plane = sb.tile([P, Q], U8, align_bytes=64)
        nc.vector.quantize_mx(
            out=states_codes[:].bitcast(FP8X4), scales=states_plane[:], in_=states_bf[:].rearrange("p q j -> p (q j)")
        )
        wq_by_group = wq_raw[:].rearrange("p (m t) -> p m t", t=PACK)
        wq_group0 = sb.tile([P, 1, P], U32, align_bytes=64)
        nc.scalar.copy(out=wq_group0[:].rearrange("p t m -> p m t"), in_=wq_by_group[:, :, 0:1])
        wq_later_groups = sb.tile([P, PACK - 1, P], U32, align_bytes=64)
        nc.vector.tensor_copy(out=wq_later_groups[:].rearrange("p t m -> p m t"), in_=wq_by_group[:, :, 1:PACK])

        qv_low = ps.tile([P, 2, Q], F32, tag="bank0")
        qv_high = ps.tile([P, 2, Q], F32, tag="bank1")
        for t in range(PACK):
            nc.tensor.matmul_mx(
                out=(qv_low, qv_high)[t // 2][:, t % 2, :],
                lhsT=(wq_group0[:, 0, :] if t == 0 else wq_later_groups[:, t - 1, :]).bitcast(FP8X4),
                lhsT_scale=wq_plane[:, t, :],
                rhs=states_codes[:].bitcast(FP8X4),
                rhs_scale=states_plane[:],
                start=True,
                stop=True,
            )
        qv_bf = sb.tile([P, Q, PACK], BF16, align_bytes=64)
        nc.vector.tensor_copy(out=qv_bf[:, :, 0:2], in_=qv_low[:].rearrange("p t q -> p q t"))
        nc.scalar.copy(out=qv_bf[:, :, 2:PACK], in_=qv_high[:].rearrange("p t q -> p q t"))
        qv_codes = sb.tile([P, Q], U32, align_bytes=64)
        qv_plane = sb.tile([P, Q], U8, align_bytes=64)
        nc.vector.quantize_mx(
            out=qv_codes[:].bitcast(FP8X4), scales=qv_plane[:], in_=qv_bf[:].rearrange("p q t -> p (q t)")
        )

        a = sb.tile([P, T], F32)
        b = sb.tile([P, U], F32)
        a_banks = []
        for piece, (lo, hi) in enumerate(A_PIECES):
            a_ps = ps.tile([P, hi - lo], F32, name="a_ps%d" % piece, tag="bank%d" % piece)
            a_banks.append(a_ps)
            nc.tensor.matmul_mx(
                out=a_ps[:],
                lhsT=qv_codes[:].bitcast(FP8X4),
                lhsT_scale=qv_plane[:],
                rhs=keys[:, lo:hi].bitcast(FP8X4),
                rhs_scale=keys_plane[:, lo:hi],
                start=True,
                stop=True,
            )
            if piece in (0, len(A_PIECES) - 1):
                nc.scalar.copy(out=a[:, lo:hi], in_=a_ps[:])
            else:
                nc.vector.tensor_copy(out=a[:, lo:hi], in_=a_ps[:])
        for piece in range(U // B_PIECE):
            cols = slice(piece * B_PIECE, (piece + 1) * B_PIECE)
            b_ps = ps.tile([P, B_PIECE], F32, name="b_ps%d" % piece)
            nc.tensor.matmul_mx(
                out=b_ps[:],
                lhsT=qv_codes[:].bitcast(FP8X4),
                lhsT_scale=qv_plane[:],
                rhs=notes[:, 2 * piece * B_PIECE : 2 * (piece + 1) * B_PIECE].bitcast(FP4X4),
                rhs_scale=notes_plane[:, cols],
                start=True,
                stop=True,
            )
            nc.vector.tensor_copy(out=b[:, cols], in_=b_ps[:])

        first = slice(0, HALF)
        second = slice(HALF, SLOTS)
        first_cols = slice(0, LIST_COLS // 2)
        second_cols = slice(LIST_COLS // 2, LIST_COLS)

        a_first = sb.tile([P, HALF], F32)
        nc.scalar.activation(a_first[:], a[:].indirect(list1[:, first_cols]), COPY)
        neg_a_second = sb.tile([P, HALF], F32)
        nc.scalar.activation(neg_a_second[:], a[:].indirect(list1[:, second_cols]), COPY, scale=-1.0)
        r = sb.tile([P, SLOTS], F32)
        nc.vector.tensor_tensor(r[:, first], b[:].indirect(list2[:, first_cols]), a_first[:], SUB)
        nc.scalar.activation(r[:, second], b[:].indirect(list2[:, second_cols]), COPY)

        nc.vector.tensor_tensor(f2[:].indirect(list2[:, second_cols]), r[:, second], neg_a_second[:], ADD)
        nc.gpsimd.tensor_tensor(r[:, second], r[:, second], neg_a_second[:], ADD)
        nc.vector.tensor_copy(f2[:].indirect(list2[:, first_cols]), r[:, first])
        nc.vector.tensor_copy(f1[:].indirect(list1[:]), r[:])

        neg_lam = sb.tile([P, 1], F32)
        nc.gpsimd.tensor_scalar(neg_lam[:], lam_col[:], -1.0, None, MULT)

        b2 = sb.tile([P, U], F32)
        nc.gpsimd.tensor_tensor(b2[:], b[:], f2[:], SUB)
        b2_listed = sb.tile([P, SLOTS], F32)
        nc.scalar.activation(b2_listed[:, first], b2[:].indirect(list4[:, first_cols]), COPY)
        weighted_first = sb.tile([P, HALF], F32)
        nc.scalar.activation(weighted_first[:], b2_listed[:, first], COPY, scale=neg_lam[:])
        nc.scalar.activation(b2_listed[:, second], b2[:].indirect(list4[:, second_cols]), COPY)

        a2 = sb.tile([P, T], F32)
        bank1_start = A_PIECES[1][0]
        nc.gpsimd.tensor_tensor(a2[:, A2_SPLIT:T], a[:, A2_SPLIT:T], f1[:, A2_SPLIT:T], ADD)
        nc.vector.tensor_tensor(a2[:, 0:bank1_start], a_banks[0][:], f1[:, 0:bank1_start], ADD)
        nc.vector.tensor_tensor(
            a2[:, bank1_start:A2_SPLIT], a_banks[1][:, 0 : A2_SPLIT - bank1_start], f1[:, bank1_start:A2_SPLIT], ADD
        )

        result = sb.tile([P, SLOTS], F32)
        nc.vector.tensor_tensor(result[:, first], a2[:].indirect(list3[:, first_cols]), weighted_first[:], ADD)
        nc.sync.dma_start(out=out[:, first], in_=result[:, first])
        a2_second = sb.tile([P, HALF], F32)
        nc.scalar.activation(a2_second[:], a2[:].indirect(list3[:, second_cols]), COPY)
        nc.vector.scalar_tensor_tensor(result[:, second], b2_listed[:, second], neg_lam[:], a2_second[:], MULT, ADD)
        nc.sync.dma_start(out=out[:, second], in_=result[:, second])
